import numpy as np
import ml_dtypes


def mxq(x, axis, fmt="e4m3"):
    dtype, down = {"e4m3": (ml_dtypes.float8_e4m3fn, 7), "e5m2": (ml_dtypes.float8_e5m2, 14)}[fmt]
    v = np.moveaxis(np.asarray(x, np.float32).astype(ml_dtypes.bfloat16).astype(np.float64), axis, -1)
    blocks = v.reshape(v.shape[:-1] + (-1, 32))
    amax = np.abs(blocks).max(-1, keepdims=True)
    byte = np.maximum(np.where(amax > 0, np.frexp(amax)[1] - 1 + 127, 0) - down, 1)
    scale = np.exp2(byte - 127.0)
    codes = (blocks / scale).astype(np.float32).astype(dtype).astype(np.float64)
    return np.moveaxis((codes * scale).reshape(v.shape), -1, axis)


WIDE = False


def mx_kscale(k):
    if not WIDE:
        return np.ones(k)
    levels = np.array([10, -10, 5, -5, 0])
    if k % 512:
        return np.exp2(np.random.permutation(np.resize(levels, k // 32))).repeat(32)
    a = np.empty((k // 512, 16))
    for p in range(k // 512):
        a[p, :8] = np.random.permutation(np.resize(levels, 8))
        for g in range(8):
            far = levels[np.abs(levels - a[p, g]) >= 10]
            a[p, g + 8] = far[np.random.randint(len(far))]
    return np.exp2(a.ravel()).repeat(32)


def f64(x):
    return np.asarray(x).astype(np.float64)


def striped(idx):
    return np.tile(idx.reshape(-1, 16).T, (8, 1)).astype(np.uint16)


def unstriped(offs):
    return offs[:16].T.reshape(-1).astype(np.int64)


E2M1 = np.array([0.0, 0.5, 1.0, 1.5, 2.0, 3.0, 4.0, 6.0, -0.0, -0.5, -1.0, -1.5, -2.0, -3.0, -4.0, -6.0])


def pack_weight(w, fmt):
    k, n = w.shape
    w = f64(np.asarray(w, np.float32).astype(ml_dtypes.bfloat16)).reshape(k // 32, 32, n)
    amax = np.abs(w).max(1)
    if fmt == "e4m3":
        byte = np.frexp(amax)[1] - 1 + 127 - 7
    else:
        mant, ex = np.frexp(amax / 6.0)
        byte = np.where(mant > 0.5, ex, ex - 1) + 127
    byte = np.clip(np.where(amax > 0, byte, 1), 1, 254)
    scaled = (w * np.exp2(127.0 - byte)[:, None, :]).reshape(k, n).astype(np.float32)
    by_word = np.ascontiguousarray(scaled.reshape(k // 512, 128, 4, n).transpose(0, 1, 3, 2))
    if fmt == "e4m3":
        words = by_word.astype(ml_dtypes.float8_e4m3fn).view(np.uint8)
    else:
        c = by_word.astype(ml_dtypes.float4_e2m1fn).view(np.uint8) & 0xF
        words = (c[..., 0::2] | (c[..., 1::2] << 4)).reshape(k // 512, 128, 2 * n)
    return np.ascontiguousarray(words), np.ascontiguousarray(byte.astype(np.uint8).reshape(k // 512, 16, n))


def unpack_weight(words, scales, fmt):
    g, _, n = scales.shape
    words = np.ascontiguousarray(words).reshape(g, 128, n, -1)
    if fmt == "e4m3":
        vals = words.view(ml_dtypes.float8_e4m3fn).astype(np.float64)
    else:
        nib = np.empty((g, 128, n, 4), np.uint8)
        nib[..., 0::2] = words & 0xF
        nib[..., 1::2] = words >> 4
        vals = E2M1[nib]
    vals = vals * np.repeat(np.exp2(scales.astype(np.float64) - 127.0), 8, axis=1)[..., None]
    return vals.transpose(0, 1, 3, 2).reshape(g * 512, n)


def pack_table(v):
    words, scales = pack_weight(v, "e4m3")
    return np.concatenate([words.reshape(words.shape[0], -1), scales.reshape(scales.shape[0], -1)], axis=1)


def unpack_table(tab):
    g, t = tab.shape[0], tab.shape[1] // 528
    return unpack_weight(tab[:, :512 * t].reshape(g, 128, t, 4), tab[:, 512 * t:].reshape(g, 16, t), "e4m3")


K, M, T, S = 1024, 512, 512, 256


def setup_inputs():
    n = np.random.standard_normal
    s = mx_kscale(K)[:, None]
    return {
        "tab": pack_table(n((K, T)) * s),
        "w": (n((K, M)) / np.sqrt(K) / s).astype(np.float32),
        "offs": striped(np.random.permutation(T)[:S]),
    }


def reference(tab, w, offs):
    tab_ = unpack_table(tab)[:, unstriped(offs)]
    w_ = mxq(f64(w), 0, "e4m3")
    y = w_.T @ tab_
    return y

@@ -1,0 +1,111 @@
+from contextlib import ExitStack
+
+import concourse.mybir as mybir
+
+K, M, T, S = 1024, 512, 512, 256
+FLOPS = 2 * K * M * S
+
+F32 = mybir.dt.float32
+BF16 = mybir.dt.bfloat16
+I32 = mybir.dt.int32
+U32 = mybir.dt.uint32
+U16 = mybir.dt.uint16
+U8 = mybir.dt.uint8
+FP8X4 = mybir.dt.float8_e4m3fn_x4
+
+P = 128
+PACK = 4
+PASSES = K // (P * PACK)
+M_TILE = 128
+WIDTH = 256
+
+
+def interleave(copy, grouped, raw, first, last):
+    copy(
+        out=grouped[:, first:last, :].rearrange("p (c i) t -> p c t i", i=4),
+        in_=raw[:, :, first:last].rearrange("p t (c i) -> p c t i", i=4),
+    )
+
+
+def tile_list_tabw_none_kernel(tc, tab, w, offs, out):
+    nc = tc.nc
+    with ExitStack() as ctx:
+        held = ctx.enter_context(tc.tile_pool(name="held", bufs=1))
+        psum = ctx.enter_context(tc.psum_pool(name="psum", bufs=1))
+
+        offsets = held.tile([P, S // 16], U16, name="offsets")
+        nc.sync.dma_start(offsets[:], offs)
+
+        tab_words = tab.bitcast(I32)
+        words = []
+        for a in range(PASSES):
+            tile = held.tile([P, T], I32, name=f"words{a}", align_bytes=64)
+            nc.sync.dma_start(tile[:], tab_words[a, 0 : P * T].rearrange("(p t) -> p t", p=P))
+            words.append(tile)
+
+        tab_scales = held.tile([P, T // 4], I32, name="tab_scales", align_bytes=64)
+        nc.vector.memset(tab_scales[:], 0)
+        row = T // 4
+        for q in range(4):
+            rows = tab_words[:, P * T + 4 * q * row : P * T + 4 * (q + 1) * row]
+            nc.sync.dma_start(tab_scales[32 * q : 32 * q + 8, :], rows.rearrange("a (r t) -> a r t", r=4))
+
+        w_rows = w.rearrange("(a p j) m -> a p j m", p=P, j=PACK)
+        raws = {}
+        for h in range(M // WIDTH):
+            for a in range(PASSES):
+                raw = held.tile([P, PACK, WIDTH], F32, name=f"raw{a}{h}", align_bytes=64)
+                nc.sync.dma_start(raw[:], w_rows[a][:, :, h * WIDTH : (h + 1) * WIDTH])
+                raws[a, h] = raw
+
+        picked = []
+        for a in range(PASSES):
+            tile = held.tile([P, S], U32, name=f"picked{a}", align_bytes=64)
+            nc.vector.tensor_copy(tile[:], words[a][:].bitcast(U32).indirect(offsets[:]))
+            picked.append(tile)
+        picked_scales = held.tile([P, S], U8, name="picked_scales", align_bytes=64)
+
+        codes = {}
+        planes = {}
+        sums = {}
+        shares = {(0, 0): (1, 128), (1, 0): (1, 144), (0, 1): (1, 144), (1, 1): (2, 80)}
+        for h in range(M // WIDTH):
+            for a in range(PASSES):
+                pieces, share = shares[a, h]
+                width = WIDTH // pieces
+                grouped = held.tile([P, WIDTH, PACK], BF16, name=f"grouped{a}{h}", align_bytes=64)
+                codes[a, h] = held.tile([P, WIDTH], U32, name=f"codes{a}{h}", align_bytes=64)
+                planes[a, h] = held.tile([P, WIDTH], U8, name=f"planes{a}{h}", align_bytes=64)
+                for i in range(pieces):
+                    interleave(nc.vector.tensor_copy, grouped, raws[a, h], i * width, i * width + share)
+                    interleave(nc.scalar.copy, grouped, raws[a, h], i * width + share, (i + 1) * width)
+                if (a, h) == (0, 0):
+                    nc.vector.tensor_copy(picked_scales[:], tab_scales[:].bitcast(U8).indirect(offsets[:]))
+                for i in range(pieces):
+                    cols = slice(i * width, (i + 1) * width)
+                    nc.vector.quantize_mx(
+                        out=codes[a, h][:, cols].bitcast(FP8X4),
+                        scales=planes[a, h][:, cols],
+                        in_=grouped[:, cols, :].rearrange("p w j -> p (w j)"),
+                    )
+                for i in range(WIDTH // M_TILE):
+                    if a == 0:
+                        sums[h, i] = psum.tile([M_TILE, S], F32, name=f"sum{h}{i}")
+                    cols = slice(i * M_TILE, (i + 1) * M_TILE)
+                    nc.tensor.matmul_mx(
+                        out=sums[h, i][:],
+                        lhsT=codes[a, h][:, cols].bitcast(FP8X4),
+                        lhsT_scale=planes[a, h][:, cols],
+                        rhs=picked[a][:].bitcast(FP8X4),
+                        rhs_scale=picked_scales[4 * a :, :],
+                        start=(a == 0),
+                        stop=(a == PASSES - 1),
+                    )
+            for i in range(WIDTH // M_TILE):
+                result = held.tile([M_TILE, S], F32, name=f"result{h}{i}")
+                if i == 0:
+                    nc.vector.tensor_copy(out=result[:], in_=sums[h, i][:])
+                else:
+                    nc.scalar.copy(out=result[:], in_=sums[h, i][:])
+                n0 = h * WIDTH + i * M_TILE
+                nc.sync.dma_start(out=out[n0 : n0 + M_TILE, :], in_=result[:])

@@ -17,7 +17,14 @@ P = 128
 PACK = 4
 PASSES = K // (P * PACK)
 M_TILE = 128
-WIDTH = 256
+CHUNKS = (
+    (0, 0, 256, ((0, 256, 112),)),
+    (1, 0, 256, ((0, 256, 112),)),
+    (0, 256, 512, ((0, 256, 112),)),
+    (1, 256, 384, ((0, 128, 64),)),
+    (1, 384, 512, ((0, 128, 72),)),
+)
+PARTS = (((0, S, "scalar"),), ((0, S, "scalar"),), ((0, S, "scalar"),), ((0, 128, "scalar"), (128, S, "vector")))
 
 
 def interleave(copy, grouped, raw, first, last):
@@ -37,75 +44,82 @@ def tile_list_tabw_none_kernel(tc, tab, w, offs, out):
         nc.sync.dma_start(offsets[:], offs)
 
         tab_words = tab.bitcast(I32)
-        words = []
-        for a in range(PASSES):
+        row = T // 4
+        w_rows = w.rearrange("(a p j) m -> a p j m", p=P, j=PACK)
+
+        def load_words(a):
             tile = held.tile([P, T], I32, name=f"words{a}", align_bytes=64)
             nc.sync.dma_start(tile[:], tab_words[a, 0 : P * T].rearrange("(p t) -> p t", p=P))
-            words.append(tile)
+            return tile
+
+        def load_chunk(i):
+            a, first, last, pieces = CHUNKS[i]
+            tile = held.tile([P, PACK, last - first], F32, name=f"raw{i}", align_bytes=64)
+            nc.sync.dma_start(tile[:], w_rows[a][:, :, first:last])
+            return tile
+
+        def pick(a, words):
+            tile = held.tile([P, S], U32, name=f"picked{a}", align_bytes=64)
+            nc.vector.tensor_copy(tile[:], words[:].bitcast(U32).indirect(offsets[:]))
+            return tile
 
         tab_scales = held.tile([P, T // 4], I32, name="tab_scales", align_bytes=64)
         nc.vector.memset(tab_scales[:], 0)
-        row = T // 4
+        words = {}
+        raws = {}
+        picked = {}
+        words[0] = load_words(0)
         for q in range(4):
             rows = tab_words[:, P * T + 4 * q * row : P * T + 4 * (q + 1) * row]
             nc.sync.dma_start(tab_scales[32 * q : 32 * q + 8, :], rows.rearrange("a (r t) -> a r t", r=4))
+        raws[0] = load_chunk(0)
+        words[1] = load_words(1)
+        raws[1] = load_chunk(1)
+        raws[2] = load_chunk(2)
+        raws[3] = load_chunk(3)
+        raws[4] = load_chunk(4)
 
-        w_rows = w.rearrange("(a p j) m -> a p j m", p=P, j=PACK)
-        raws = {}
-        for h in range(M // WIDTH):
-            for a in range(PASSES):
-                raw = held.tile([P, PACK, WIDTH], F32, name=f"raw{a}{h}", align_bytes=64)
-                nc.sync.dma_start(raw[:], w_rows[a][:, :, h * WIDTH : (h + 1) * WIDTH])
-                raws[a, h] = raw
-
-        picked = []
-        for a in range(PASSES):
-            tile = held.tile([P, S], U32, name=f"picked{a}", align_bytes=64)
-            nc.vector.tensor_copy(tile[:], words[a][:].bitcast(U32).indirect(offsets[:]))
-            picked.append(tile)
+        picked[0] = pick(0, words[0])
         picked_scales = held.tile([P, S], U8, name="picked_scales", align_bytes=64)
-
-        codes = {}
-        planes = {}
+        nc.vector.tensor_copy(picked_scales[:], tab_scales[:].bitcast(U8).indirect(offsets[:]))
         sums = {}
-        shares = {(0, 0): (1, 128), (1, 0): (1, 144), (0, 1): (1, 144), (1, 1): (2, 80)}
-        for h in range(M // WIDTH):
-            for a in range(PASSES):
-                pieces, share = shares[a, h]
-                width = WIDTH // pieces
-                grouped = held.tile([P, WIDTH, PACK], BF16, name=f"grouped{a}{h}", align_bytes=64)
-                codes[a, h] = held.tile([P, WIDTH], U32, name=f"codes{a}{h}", align_bytes=64)
-                planes[a, h] = held.tile([P, WIDTH], U8, name=f"planes{a}{h}", align_bytes=64)
-                for i in range(pieces):
-                    interleave(nc.vector.tensor_copy, grouped, raws[a, h], i * width, i * width + share)
-                    interleave(nc.scalar.copy, grouped, raws[a, h], i * width + share, (i + 1) * width)
-                if (a, h) == (0, 0):
-                    nc.vector.tensor_copy(picked_scales[:], tab_scales[:].bitcast(U8).indirect(offsets[:]))
-                for i in range(pieces):
-                    cols = slice(i * width, (i + 1) * width)
-                    nc.vector.quantize_mx(
-                        out=codes[a, h][:, cols].bitcast(FP8X4),
-                        scales=planes[a, h][:, cols],
-                        in_=grouped[:, cols, :].rearrange("p w j -> p (w j)"),
-                    )
-                for i in range(WIDTH // M_TILE):
+        for c, (a, first, last, pieces) in enumerate(CHUNKS):
+            raw = raws[c]
+            width = last - first
+            grouped = held.tile([P, width, PACK], BF16, name=f"grouped{c}", align_bytes=64)
+            codes = held.tile([P, width], U32, name=f"codes{c}", align_bytes=64)
+            plane = held.tile([P, width], U8, name=f"plane{c}", align_bytes=64)
+            for begin, end, share in pieces:
+                interleave(nc.vector.tensor_copy, grouped, raw, begin, begin + share)
+                interleave(nc.scalar.copy, grouped, raw, begin + share, end)
+            if c == 0:
+                picked[1] = pick(1, words[1])
+            for begin, end, share in pieces:
+                nc.vector.quantize_mx(
+                    out=codes[:, begin:end].bitcast(FP8X4),
+                    scales=plane[:, begin:end],
+                    in_=grouped[:, begin:end, :].rearrange("p w j -> p (w j)"),
+                )
+            for m in range(first // M_TILE, last // M_TILE):
+                cols = slice(m * M_TILE - first, (m + 1) * M_TILE - first)
+                for begin, end, copy in PARTS[m]:
                     if a == 0:
-                        sums[h, i] = psum.tile([M_TILE, S], F32, name=f"sum{h}{i}")
-                    cols = slice(i * M_TILE, (i + 1) * M_TILE)
+                        sums[m, begin] = psum.tile([M_TILE, end - begin], F32, name=f"sum{m}_{begin}")
                     nc.tensor.matmul_mx(
-                        out=sums[h, i][:],
-                        lhsT=codes[a, h][:, cols].bitcast(FP8X4),
-                        lhsT_scale=planes[a, h][:, cols],
-                        rhs=picked[a][:].bitcast(FP8X4),
-                        rhs_scale=picked_scales[4 * a :, :],
+                        out=sums[m, begin][:],
+                        lhsT=codes[:, cols].bitcast(FP8X4),
+                        lhsT_scale=plane[:, cols],
+                        rhs=picked[a][:, begin:end].bitcast(FP8X4),
+                        rhs_scale=picked_scales[4 * a :, begin:end],
                         start=(a == 0),
                         stop=(a == PASSES - 1),
                     )
-            for i in range(WIDTH // M_TILE):
-                result = held.tile([M_TILE, S], F32, name=f"result{h}{i}")
-                if i == 0:
-                    nc.vector.tensor_copy(out=result[:], in_=sums[h, i][:])
-                else:
-                    nc.scalar.copy(out=result[:], in_=sums[h, i][:])
-                n0 = h * WIDTH + i * M_TILE
-                nc.sync.dma_start(out=out[n0 : n0 + M_TILE, :], in_=result[:])
+            if a == PASSES - 1:
+                for m in range(first // M_TILE, last // M_TILE):
+                    result = held.tile([M_TILE, S], F32, name=f"result{m}")
+                    for begin, end, copy in PARTS[m]:
+                        if copy == "vector":
+                            nc.vector.tensor_copy(out=result[:, begin:end], in_=sums[m, begin][:])
+                        else:
+                            nc.scalar.copy(out=result[:, begin:end], in_=sums[m, begin][:])
+                    nc.sync.dma_start(out=out[m * M_TILE : (m + 1) * M_TILE, :], in_=result[:])

from contextlib import ExitStack

import concourse.mybir as mybir

K, M, T, S = 1024, 512, 512, 256
FLOPS = 2 * K * M * S

F32 = mybir.dt.float32
BF16 = mybir.dt.bfloat16
I32 = mybir.dt.int32
U32 = mybir.dt.uint32
U16 = mybir.dt.uint16
U8 = mybir.dt.uint8
FP8X4 = mybir.dt.float8_e4m3fn_x4

P = 128
PACK = 4
PASSES = K // (P * PACK)
M_TILE = 128
CHUNKS = (
    (0, 0, 256, ((0, 256, 112),)),
    (1, 0, 256, ((0, 256, 112),)),
    (0, 256, 512, ((0, 256, 112),)),
    (1, 256, 384, ((0, 128, 64),)),
    (1, 384, 512, ((0, 128, 72),)),
)
PARTS = (((0, S, "scalar"),), ((0, S, "scalar"),), ((0, S, "scalar"),), ((0, 128, "scalar"), (128, S, "vector")))


def interleave(copy, grouped, raw, first, last):
    copy(
        out=grouped[:, first:last, :].rearrange("p (c i) t -> p c t i", i=4),
        in_=raw[:, :, first:last].rearrange("p t (c i) -> p c t i", i=4),
    )


def tile_list_tabw_none_kernel(tc, tab, w, offs, out):
    nc = tc.nc
    with ExitStack() as ctx:
        held = ctx.enter_context(tc.tile_pool(name="held", bufs=1))
        psum = ctx.enter_context(tc.psum_pool(name="psum", bufs=1))

        offsets = held.tile([P, S // 16], U16, name="offsets")
        nc.sync.dma_start(offsets[:], offs)

        tab_words = tab.bitcast(I32)
        row = T // 4
        w_rows = w.rearrange("(a p j) m -> a p j m", p=P, j=PACK)

        def load_words(a):
            tile = held.tile([P, T], I32, name=f"words{a}", align_bytes=64)
            nc.sync.dma_start(tile[:], tab_words[a, 0 : P * T].rearrange("(p t) -> p t", p=P))
            return tile

        def load_chunk(i):
            a, first, last, pieces = CHUNKS[i]
            tile = held.tile([P, PACK, last - first], F32, name=f"raw{i}", align_bytes=64)
            nc.sync.dma_start(tile[:], w_rows[a][:, :, first:last])
            return tile

        def pick(a, words):
            tile = held.tile([P, S], U32, name=f"picked{a}", align_bytes=64)
            nc.vector.tensor_copy(tile[:], words[:].bitcast(U32).indirect(offsets[:]))
            return tile

        tab_scales = held.tile([P, T // 4], I32, name="tab_scales", align_bytes=64)
        nc.vector.memset(tab_scales[:], 0)
        words = {}
        raws = {}
        picked = {}
        words[0] = load_words(0)
        for q in range(4):
            rows = tab_words[:, P * T + 4 * q * row : P * T + 4 * (q + 1) * row]
            nc.sync.dma_start(tab_scales[32 * q : 32 * q + 8, :], rows.rearrange("a (r t) -> a r t", r=4))
        raws[0] = load_chunk(0)
        words[1] = load_words(1)
        raws[1] = load_chunk(1)
        raws[2] = load_chunk(2)
        raws[3] = load_chunk(3)
        raws[4] = load_chunk(4)

        picked[0] = pick(0, words[0])
        picked_scales = held.tile([P, S], U8, name="picked_scales", align_bytes=64)
        nc.vector.tensor_copy(picked_scales[:], tab_scales[:].bitcast(U8).indirect(offsets[:]))
        sums = {}
        for c, (a, first, last, pieces) in enumerate(CHUNKS):
            raw = raws[c]
            width = last - first
            grouped = held.tile([P, width, PACK], BF16, name=f"grouped{c}", align_bytes=64)
            codes = held.tile([P, width], U32, name=f"codes{c}", align_bytes=64)
            plane = held.tile([P, width], U8, name=f"plane{c}", align_bytes=64)
            for begin, end, share in pieces:
                interleave(nc.vector.tensor_copy, grouped, raw, begin, begin + share)
                interleave(nc.scalar.copy, grouped, raw, begin + share, end)
            if c == 0:
                picked[1] = pick(1, words[1])
            for begin, end, share in pieces:
                nc.vector.quantize_mx(
                    out=codes[:, begin:end].bitcast(FP8X4),
                    scales=plane[:, begin:end],
                    in_=grouped[:, begin:end, :].rearrange("p w j -> p (w j)"),
                )
            for m in range(first // M_TILE, last // M_TILE):
                cols = slice(m * M_TILE - first, (m + 1) * M_TILE - first)
                for begin, end, copy in PARTS[m]:
                    if a == 0:
                        sums[m, begin] = psum.tile([M_TILE, end - begin], F32, name=f"sum{m}_{begin}")
                    nc.tensor.matmul_mx(
                        out=sums[m, begin][:],
                        lhsT=codes[:, cols].bitcast(FP8X4),
                        lhsT_scale=plane[:, cols],
                        rhs=picked[a][:, begin:end].bitcast(FP8X4),
                        rhs_scale=picked_scales[4 * a :, begin:end],
                        start=(a == 0),
                        stop=(a == PASSES - 1),
                    )
            if a == PASSES - 1:
                for m in range(first // M_TILE, last // M_TILE):
                    result = held.tile([M_TILE, S], F32, name=f"result{m}")
                    for begin, end, copy in PARTS[m]:
                        if copy == "vector":
                            nc.vector.tensor_copy(out=result[:, begin:end], in_=sums[m, begin][:])
                        else:
                            nc.scalar.copy(out=result[:, begin:end], in_=sums[m, begin][:])
                    nc.sync.dma_start(out=out[m * M_TILE : (m + 1) * M_TILE, :], in_=result[:])
